import numpy as np, ml_dtypes
CORES = [5,13,21,29,37,45,53,61,253,245,237,229,221,213,205,197]
N = 16
GROUPS = [[0,8],[1,9],[2,10],[3,11],[4,12],[5,13],[6,14],[7,15]]
def setup_inputs(rng):
    return {"x": rng.standard_normal((N, 128, 1024), dtype=np.float32).astype(ml_dtypes.bfloat16)}
def reference(x):
    y = np.empty((N, 128, 1024), x.dtype)
    for g in GROUPS:
        s = x[g].max(axis=0)
        for r in g:
            y[r] = s
    return {"y": y}

@@ -1,0 +1,81 @@
+import concourse.bass as bass
+
+NP = 4
+GL = 1
+GW = 1
+GO = 1
+HELP = (2, 6, 3, 7)
+ROWS = 128 // NP
+W = ROWS * 8
+
+SCRATCH = {
+    "xin": ("dram", [NP, 128, W], "bfloat16"),
+    "res": ("dram", [NP, 128, W], "bfloat16"),
+}
+SEMAPHORES = ["ld0", "ld1", "ld2", "ld3", "ld4", "ld5", "ld6", "ld7",
+              "own0", "own1", "own2", "own3", "peer0", "peer1", "peer2", "peer3",
+              "res0", "res1", "res2", "res3", "res4", "res5", "res6", "res7",
+              "st", "sent"]
+
+
+def rank_program(g, core, T, topo):
+    S = T.sem
+    ld = [S.ld0, S.ld1, S.ld2, S.ld3, S.ld4, S.ld5, S.ld6, S.ld7]
+    own = [S.own0, S.own1, S.own2, S.own3]
+    peer = [S.peer0, S.peer1, S.peer2, S.peer3]
+    res = [S.res0, S.res1, S.res2, S.res3, S.res4, S.res5, S.res6, S.res7]
+
+    home = {}
+    for c in T.cores:
+        home[c - c % 8] = c
+    base = core - core % 8
+    if base not in home:
+        return
+    me = home[base]
+    rank = T.rank_of(me)
+    partner = None
+    for grp in T.tables["GROUPS"]:
+        if rank in grp:
+            partner = T.cores[[r for r in grp if r != rank][0]]
+    eng = 16 // GW
+
+    if core == me:
+        for l in range(NP // GL):
+            dst = T.xin[l] if GL == 1 else T.xin[l * GL:(l + 1) * GL]
+            g.dma_start(dst, T.x[l * GL * ROWS:(l + 1) * GL * ROWS, :]).then_inc(ld[l], 16)
+        seen = 0
+        for w in range(NP // GW):
+            while seen * GL < (w + 1) * GW:
+                g.wait_ge(ld[seen], 16)
+                seen += 1
+            trs = []
+            for i in range(GW):
+                p = w * GW + i
+                rid, pid = topo.addr(base + HELP[p % 4], core)
+                trs.append(bass.RemoteDMATransfer(
+                    dst_ids=[bass.DstId(rid=rid, pnc=pid)], dma_engine_mask=((1 << eng) - 1) << (i * eng),
+                    remote_sem=own[p // 4], src=T.xin[p], dst=T.xin[p]))
+            g.remote_dma_fused(trs, local_sem=S.sent)
+        for o in range(NP // GO):
+            g.wait_ge(res[o], 16 * GO)
+            src = T.res[o] if GO == 1 else T.res[o * GO:(o + 1) * GO]
+            g.dma_start(T.y[o * GO * ROWS:(o + 1) * GO * ROWS, :], src).then_inc(S.st, 16)
+        g.wait_ge(S.sent, 16 * (NP // GW))
+        g.wait_ge(S.st, 16 * (NP // GO))
+        return
+
+    if core % 8 not in HELP:
+        return
+    mine = [p for p in range(NP) if HELP[p % 4] == core % 8]
+    rid, pid = topo.addr(partner - partner % 8 + core % 8, core)
+    for p in mine:
+        g.wait_ge(own[p // 4], eng)
+        g.remote_dma(out_ap=T.res[p], in_ap=T.xin[p], remote_sem=peer[p // 4], local_sem=S.sent,
+                     pid=pid, routing_id=rid, dma_engine_mask=0x00FF)
+    rid, pid = topo.addr(me, core)
+    for p in mine:
+        g.wait_ge(peer[p // 4], 8)
+        g.remote_dma_fused([bass.RemoteDMATransfer(
+            dst_ids=[bass.DstId(rid=rid, pnc=pid)], dma_engine_mask=0xFFFF, remote_sem=res[p // GO],
+            srcs=[T.xin[p], T.res[p]], dsts=[T.res[p]], alu_op=2)], local_sem=S.sent)
+    g.wait_ge(S.sent, 24 * len(mine))

@@ -1,9 +1,9 @@
 import concourse.bass as bass
 
 NP = 4
-GL = 1
-GW = 1
-GO = 1
+GL = 4
+GW = 4
+GO = 4
 HELP = (2, 6, 3, 7)
 ROWS = 128 // NP
 W = ROWS * 8

@@ -1,9 +1,9 @@
 import concourse.bass as bass
 
 NP = 4
-GL = 4
-GW = 4
-GO = 4
+GL = 2
+GW = 2
+GO = 2
 HELP = (2, 6, 3, 7)
 ROWS = 128 // NP
 W = ROWS * 8

@@ -1,9 +1,9 @@
 import concourse.bass as bass
 
-NP = 4
-GL = 2
-GW = 2
-GO = 2
+NP = 8
+GL = 4
+GW = 4
+GO = 4
 HELP = (2, 6, 3, 7)
 ROWS = 128 // NP
 W = ROWS * 8

@@ -1,29 +1,25 @@
 import concourse.bass as bass
 
 NP = 8
-GL = 4
-GW = 4
-GO = 4
+GR = 4
 HELP = (2, 6, 3, 7)
 ROWS = 128 // NP
 W = ROWS * 8
+ENG = 16 // GR
 
 SCRATCH = {
     "xin": ("dram", [NP, 128, W], "bfloat16"),
     "res": ("dram", [NP, 128, W], "bfloat16"),
 }
-SEMAPHORES = ["ld0", "ld1", "ld2", "ld3", "ld4", "ld5", "ld6", "ld7",
-              "own0", "own1", "own2", "own3", "peer0", "peer1", "peer2", "peer3",
-              "res0", "res1", "res2", "res3", "res4", "res5", "res6", "res7",
-              "st", "sent"]
+SEMAPHORES = ["ld0", "ld1", "own0", "own1", "peer0", "peer1", "res0", "res1", "st", "sent"]
 
 
 def rank_program(g, core, T, topo):
     S = T.sem
-    ld = [S.ld0, S.ld1, S.ld2, S.ld3, S.ld4, S.ld5, S.ld6, S.ld7]
-    own = [S.own0, S.own1, S.own2, S.own3]
-    peer = [S.peer0, S.peer1, S.peer2, S.peer3]
-    res = [S.res0, S.res1, S.res2, S.res3, S.res4, S.res5, S.res6, S.res7]
+    ld = [S.ld0, S.ld1]
+    own = [S.own0, S.own1]
+    peer = [S.peer0, S.peer1]
+    res = [S.res0, S.res1]
 
     home = {}
     for c in T.cores:
@@ -37,31 +33,26 @@ def rank_program(g, core, T, topo):
     for grp in T.tables["GROUPS"]:
         if rank in grp:
             partner = T.cores[[r for r in grp if r != rank][0]]
-    eng = 16 // GW
+    rounds = NP // GR
 
     if core == me:
-        for l in range(NP // GL):
-            dst = T.xin[l] if GL == 1 else T.xin[l * GL:(l + 1) * GL]
-            g.dma_start(dst, T.x[l * GL * ROWS:(l + 1) * GL * ROWS, :]).then_inc(ld[l], 16)
-        seen = 0
-        for w in range(NP // GW):
-            while seen * GL < (w + 1) * GW:
-                g.wait_ge(ld[seen], 16)
-                seen += 1
+        for r in range(rounds):
+            g.dma_start(T.xin[r * GR:(r + 1) * GR], T.x[r * GR * ROWS:(r + 1) * GR * ROWS, :]).then_inc(ld[r], 16)
+        for r in range(rounds):
+            g.wait_ge(ld[r], 16)
             trs = []
-            for i in range(GW):
-                p = w * GW + i
-                rid, pid = topo.addr(base + HELP[p % 4], core)
+            for i in range(GR):
+                p = r * GR + i
+                rid, pid = topo.addr(base + HELP[i], core)
                 trs.append(bass.RemoteDMATransfer(
-                    dst_ids=[bass.DstId(rid=rid, pnc=pid)], dma_engine_mask=((1 << eng) - 1) << (i * eng),
-                    remote_sem=own[p // 4], src=T.xin[p], dst=T.xin[p]))
+                    dst_ids=[bass.DstId(rid=rid, pnc=pid)], dma_engine_mask=((1 << ENG) - 1) << (i * ENG),
+                    remote_sem=own[r], src=T.xin[p], dst=T.xin[p]))
             g.remote_dma_fused(trs, local_sem=S.sent)
-        for o in range(NP // GO):
-            g.wait_ge(res[o], 16 * GO)
-            src = T.res[o] if GO == 1 else T.res[o * GO:(o + 1) * GO]
-            g.dma_start(T.y[o * GO * ROWS:(o + 1) * GO * ROWS, :], src).then_inc(S.st, 16)
-        g.wait_ge(S.sent, 16 * (NP // GW))
-        g.wait_ge(S.st, 16 * (NP // GO))
+        for r in range(rounds):
+            g.wait_ge(res[r], 16 * GR)
+            g.dma_start(T.y[r * GR * ROWS:(r + 1) * GR * ROWS, :], T.res[r * GR:(r + 1) * GR]).then_inc(S.st, 16)
+        g.wait_ge(S.sent, 16 * rounds)
+        g.wait_ge(S.st, 16 * rounds)
         return
 
     if core % 8 not in HELP:
@@ -69,13 +60,13 @@ def rank_program(g, core, T, topo):
     mine = [p for p in range(NP) if HELP[p % 4] == core % 8]
     rid, pid = topo.addr(partner - partner % 8 + core % 8, core)
     for p in mine:
-        g.wait_ge(own[p // 4], eng)
-        g.remote_dma(out_ap=T.res[p], in_ap=T.xin[p], remote_sem=peer[p // 4], local_sem=S.sent,
+        g.wait_ge(own[p // GR], ENG)
+        g.remote_dma(out_ap=T.res[p], in_ap=T.xin[p], remote_sem=peer[p // GR], local_sem=S.sent,
                      pid=pid, routing_id=rid, dma_engine_mask=0x00FF)
     rid, pid = topo.addr(me, core)
     for p in mine:
-        g.wait_ge(peer[p // 4], 8)
+        g.wait_ge(peer[p // GR], 8)
         g.remote_dma_fused([bass.RemoteDMATransfer(
-            dst_ids=[bass.DstId(rid=rid, pnc=pid)], dma_engine_mask=0xFFFF, remote_sem=res[p // GO],
+            dst_ids=[bass.DstId(rid=rid, pnc=pid)], dma_engine_mask=0xFFFF, remote_sem=res[p // GR],
             srcs=[T.xin[p], T.res[p]], dsts=[T.res[p]], alu_op=2)], local_sem=S.sent)
     g.wait_ge(S.sent, 24 * len(mine))

import concourse.bass as bass

NP = 8
GR = 4
HELP = (2, 6, 3, 7)
ROWS = 128 // NP
W = ROWS * 8
ENG = 16 // GR

SCRATCH = {
    "xin": ("dram", [NP, 128, W], "bfloat16"),
    "res": ("dram", [NP, 128, W], "bfloat16"),
}
SEMAPHORES = ["ld0", "ld1", "own0", "own1", "peer0", "peer1", "res0", "res1", "st", "sent"]


def rank_program(g, core, T, topo):
    S = T.sem
    ld = [S.ld0, S.ld1]
    own = [S.own0, S.own1]
    peer = [S.peer0, S.peer1]
    res = [S.res0, S.res1]

    home = {}
    for c in T.cores:
        home[c - c % 8] = c
    base = core - core % 8
    if base not in home:
        return
    me = home[base]
    rank = T.rank_of(me)
    partner = None
    for grp in T.tables["GROUPS"]:
        if rank in grp:
            partner = T.cores[[r for r in grp if r != rank][0]]
    rounds = NP // GR

    if core == me:
        for r in range(rounds):
            g.dma_start(T.xin[r * GR:(r + 1) * GR], T.x[r * GR * ROWS:(r + 1) * GR * ROWS, :]).then_inc(ld[r], 16)
        for r in range(rounds):
            g.wait_ge(ld[r], 16)
            trs = []
            for i in range(GR):
                p = r * GR + i
                rid, pid = topo.addr(base + HELP[i], core)
                trs.append(bass.RemoteDMATransfer(
                    dst_ids=[bass.DstId(rid=rid, pnc=pid)], dma_engine_mask=((1 << ENG) - 1) << (i * ENG),
                    remote_sem=own[r], src=T.xin[p], dst=T.xin[p]))
            g.remote_dma_fused(trs, local_sem=S.sent)
        for r in range(rounds):
            g.wait_ge(res[r], 16 * GR)
            g.dma_start(T.y[r * GR * ROWS:(r + 1) * GR * ROWS, :], T.res[r * GR:(r + 1) * GR]).then_inc(S.st, 16)
        g.wait_ge(S.sent, 16 * rounds)
        g.wait_ge(S.st, 16 * rounds)
        return

    if core % 8 not in HELP:
        return
    mine = [p for p in range(NP) if HELP[p % 4] == core % 8]
    rid, pid = topo.addr(partner - partner % 8 + core % 8, core)
    for p in mine:
        g.wait_ge(own[p // GR], ENG)
        g.remote_dma(out_ap=T.res[p], in_ap=T.xin[p], remote_sem=peer[p // GR], local_sem=S.sent,
                     pid=pid, routing_id=rid, dma_engine_mask=0x00FF)
    rid, pid = topo.addr(me, core)
    for p in mine:
        g.wait_ge(peer[p // GR], 8)
        g.remote_dma_fused([bass.RemoteDMATransfer(
            dst_ids=[bass.DstId(rid=rid, pnc=pid)], dma_engine_mask=0xFFFF, remote_sem=res[p // GR],
            srcs=[T.xin[p], T.res[p]], dsts=[T.res[p]], alu_op=2)], local_sem=S.sent)
    g.wait_ge(S.sent, 24 * len(mine))
